import numpy as np
import ml_dtypes


def mxq(x, axis, fmt="e4m3"):
    dtype, down = {"e4m3": (ml_dtypes.float8_e4m3fn, 7), "e5m2": (ml_dtypes.float8_e5m2, 14)}[fmt]
    v = np.moveaxis(np.asarray(x, np.float32).astype(ml_dtypes.bfloat16).astype(np.float64), axis, -1)
    blocks = v.reshape(v.shape[:-1] + (-1, 32))
    amax = np.abs(blocks).max(-1, keepdims=True)
    byte = np.maximum(np.where(amax > 0, np.frexp(amax)[1] - 1 + 127, 0) - down, 1)
    scale = np.exp2(byte - 127.0)
    codes = (blocks / scale).astype(np.float32).astype(dtype).astype(np.float64)
    return np.moveaxis((codes * scale).reshape(v.shape), -1, axis)


WIDE = False


def mx_kscale(k):
    if not WIDE:
        return np.ones(k)
    levels = np.array([10, -10, 5, -5, 0])
    if k % 512:
        return np.exp2(np.random.permutation(np.resize(levels, k // 32))).repeat(32)
    a = np.empty((k // 512, 16))
    for p in range(k // 512):
        a[p, :8] = np.random.permutation(np.resize(levels, 8))
        for g in range(8):
            far = levels[np.abs(levels - a[p, g]) >= 10]
            a[p, g + 8] = far[np.random.randint(len(far))]
    return np.exp2(a.ravel()).repeat(32)


def f64(x):
    return np.asarray(x).astype(np.float64)


def striped(idx):
    return np.tile(idx.reshape(-1, 16).T, (8, 1)).astype(np.uint16)


def unstriped(offs):
    return offs[:16].T.reshape(-1).astype(np.int64)


def striped8(idx):
    return np.concatenate([x.reshape(-1, 16).T for x in idx]).astype(np.uint16)


def runs(offs, k):
    lists = np.stack([offs[16 * r : 16 * r + 16].T.reshape(-1) for r in range(8)]).astype(np.int64)
    return lists[np.arange(k) % 512 // 64]


def pack_weight(w):
    k, n = w.shape
    w = f64(np.asarray(w, np.float32).astype(ml_dtypes.bfloat16)).reshape(k // 32, 32, n)
    amax = np.abs(w).max(1)
    byte = np.clip(np.where(amax > 0, np.frexp(amax)[1] - 1 + 127 - 7, 1), 1, 254)
    scaled = (w * np.exp2(127.0 - byte)[:, None, :]).reshape(k, n).astype(np.float32)
    words = np.ascontiguousarray(scaled.reshape(k // 512, 128, 4, n).transpose(0, 1, 3, 2)).astype(ml_dtypes.float8_e4m3fn).view(np.uint8)
    return words, np.ascontiguousarray(byte.astype(np.uint8).reshape(k // 512, 16, n))


def unpack_weight(words, scales):
    g, p, n, _ = words.shape
    vals = np.ascontiguousarray(words).view(ml_dtypes.float8_e4m3fn).astype(np.float64) * np.repeat(np.exp2(scales.astype(np.float64) - 127.0), 8, axis=1)[..., None]
    return vals.transpose(0, 1, 3, 2).reshape(g * 512, n)


def sigmoid(v):
    return 1.0 / (1.0 + np.exp(-np.maximum(v, -700.0)))


K, T, S, H, C = 512, 2048, 512, 512, 512


def setup_inputs():
    n = np.random.standard_normal
    s = mx_kscale(K)[:, None]
    packed_xT = pack_weight(n((K, T)) * s)
    return {
        "x_words": packed_xT[0],
        "x_scales": packed_xT[1],
        "w1": (n((K, H)) / np.sqrt(K) / s).astype(np.float32),
        "w2": (n((K, H)) / np.sqrt(K) / s).astype(np.float32),
        "sl": np.random.uniform(1.0, 2.0, (H, 1)).astype(np.float32),
        "th": (0.5 * n((H, 1))).astype(np.float32),
        "gs": (np.random.uniform(0.5, 1.5, (K, 1)) / s).astype(np.float32),
        "tau": np.random.uniform(0.3, 0.9, (C, 1)).astype(np.float32),
        "offs": striped(np.random.permutation(T)[:S]),
        "two": striped(np.random.permutation(T)[:S]),
        "n1": striped(np.random.permutation(S)),
        "n2": striped(np.random.permutation(S)),
        "cand": striped(np.random.permutation(T)[:C]),
        "n3": striped8(np.stack([np.random.permutation(S) for _ in range(8)])),
        "n4": striped8(np.stack([np.random.permutation(S) for _ in range(8)])),
    }


def reference(x_words, x_scales, w1, w2, sl, th, gs, tau, offs, two, n1, n2, cand, n3, n4):
    x_cand = unpack_weight(x_words, x_scales)[:, unstriped(cand)]
    xq = unpack_weight(x_words, x_scales)[:, unstriped(offs)]
    y = mxq(f64(w1), 0, "e4m3").T @ xq
    x_two = unpack_weight(x_words, x_scales)[:, unstriped(two)]
    d = mxq(f64(w2), 0, "e4m3").T @ x_two
    sg = sigmoid(f64(sl) * (d[:, unstriped(n1)] - f64(th)))
    z = f64(gs) * (np.maximum(y * sg, d[:, unstriped(n2)] - d))
    s = 0.0625 * ((x_cand.T @ mxq(z, 0, "e4m3")))
    top = s.max(axis=1, keepdims=True)
    ea = np.exp(f64(tau) * (s[np.arange(C)[:, None], runs(n4, C)] - top))
    return (0.5 * (s - (s[np.arange(C)[:, None], runs(n3, C)]))) / (ea + 0.25)

@@ -1,0 +1,251 @@
+from contextlib import ExitStack
+
+import concourse.mybir as mybir
+
+K, T, S, H, C = 512, 2048, 512, 512, 512
+FLOPS = 3 * 2 * 512 * 512 * 512
+
+F32 = mybir.dt.float32
+BF16 = mybir.dt.bfloat16
+I32 = mybir.dt.int32
+U32 = mybir.dt.uint32
+U16 = mybir.dt.uint16
+U8 = mybir.dt.uint8
+FP8X4 = mybir.dt.float8_e4m3fn_x4
+ALU = mybir.AluOpType
+ACT = mybir.ActivationFunctionType
+
+P = 128
+PACK = 4
+HALF = S // 2
+HCOLS = HALF // 16
+
+
+def tile_picked_twcmxbera_none_p_kernel(
+    tc, x_words, x_scales, w1, w2, sl, th, gs, tau, offs, two, n1, n2, cand, n3, n4, out
+):
+    nc = tc.nc
+    with ExitStack() as ctx:
+        keep = ctx.enter_context(tc.tile_pool(name="keep", bufs=1))
+        psum = ctx.enter_context(tc.psum_pool(name="psum", bufs=1))
+
+        def load_list(src, name):
+            tile = keep.tile([P, S // 16], U16, name=name)
+            nc.sync.dma_start(tile[:], src)
+            return tile
+
+        def load_column(src, name):
+            tile = keep.tile([P, PACK], F32, name=name)
+            nc.gpsimd.dma_start(tile[:], src.rearrange("(p t) o -> p (t o)", t=PACK))
+            return tile
+
+        def load_weight(src, name):
+            tile = keep.tile([P, PACK, src.shape[1]], F32, name=name, tag=name, align_bytes=64)
+            nc.sync.dma_start(tile[:], src.rearrange("(p j) h -> p j h", j=PACK))
+            return tile
+
+        bytes_all = keep.tile([P, T], U8, name="bytes_all", align_bytes=64)
+        nc.gpsimd.memset(bytes_all[:].bitcast(I32), 0)
+        two_l = load_list(two, "two_l")
+        for q in range(4):
+            nc.scalar.dma_start(
+                bytes_all[32 * q : 32 * q + 4, :].bitcast(I32),
+                x_scales[0, 4 * q : 4 * q + 4, :].bitcast(I32),
+            )
+        w2_raw = [load_weight(w2[:, u * (H // 2) : (u + 1) * (H // 2)], f"w2_raw{u}") for u in range(2)]
+        offs_l = load_list(offs, "offs_l")
+        cand_l = load_list(cand, "cand_l")
+        words_all = keep.tile([P, T], I32, name="words_all", align_bytes=64)
+        nc.sync.dma_start(words_all[:], x_words[0].rearrange("p c r -> p (c r)").bitcast(I32))
+        n1_l = load_list(n1, "n1_l")
+        n2_l = load_list(n2, "n2_l")
+        w1_raw = [load_weight(w1[:, u * (H // 2) : (u + 1) * (H // 2)], f"w1_raw{u}") for u in range(2)]
+        n4_l = load_list(n4, "n4_l")
+        n3_l = load_list(n3, "n3_l")
+        sl_c = load_column(sl, "sl_c")
+        th_c = load_column(th, "th_c")
+        gs_c = load_column(gs, "gs_c")
+        tau_c = load_column(tau, "tau_c")
+
+        quarter = keep.tile([P, 1], F32, name="quarter")
+        nc.gpsimd.memset(quarter[:], 0.25)
+        slth = keep.tile([P, PACK], F32, name="slth")
+        nc.gpsimd.tensor_tensor(slth[:], sl_c[:], th_c[:], ALU.mult)
+        sg_bias = keep.tile([P, PACK], F32, name="sg_bias")
+        nc.gpsimd.tensor_scalar(sg_bias[:], slth[:], -1.0, 0.0, ALU.mult, ALU.add)
+        neg_tau = keep.tile([P, PACK], F32, name="neg_tau")
+        nc.gpsimd.tensor_scalar(neg_tau[:], tau_c[:], -1.0, 0.0, ALU.mult, ALU.add)
+
+        def gather_bytes(lst, name, dealt, tag):
+            tile = keep.tile([P, S], U8, name=name, align_bytes=64, tag=tag)
+            dst = tile[:].rearrange("p (t m) -> p m t", t=PACK) if dealt else tile[:]
+            nc.vector.tensor_copy(dst, bytes_all[:].indirect(lst[:]))
+            return tile
+
+        def gather_words(lst, name, dealt, tag):
+            tile = keep.tile([P, S], U32, name=name, align_bytes=64, tag=tag)
+            dst = tile[:].rearrange("p (t m) -> p m t", t=PACK) if dealt else tile[:]
+            nc.vector.tensor_copy(dst, words_all[:].bitcast(U32).indirect(lst[:]))
+            return tile
+
+        def dealt_view(grouped):
+            return grouped[:].rearrange("p (t m j) -> p m j t", t=PACK, j=PACK)
+
+        def raw_view(raw):
+            return raw[:].rearrange("p j (m t) -> p m j t", t=PACK)
+
+        def quantize(grouped, width, name):
+            codes = keep.tile([P, width], U32, name=name + "_codes", align_bytes=64)
+            scales = keep.tile([P, width], U8, name=name + "_scales", align_bytes=64)
+            nc.vector.quantize_mx(out=codes[:].bitcast(FP8X4), scales=scales[:], in_=grouped[:])
+            return codes, scales
+
+        def product(acc, lhs, t, rhs):
+            cols = slice(P * t, P * (t + 1))
+            nc.tensor.matmul_mx(
+                out=acc,
+                lhsT=lhs[0][:, cols].bitcast(FP8X4),
+                lhsT_scale=lhs[1][:, cols],
+                rhs=rhs[0][:].bitcast(FP8X4),
+                rhs_scale=rhs[1][:],
+                start=True,
+                stop=True,
+            )
+
+        two_b = gather_bytes(two_l, "two_b", False, "two_b")
+        offs_b = gather_bytes(offs_l, "offs_b", False, "offs_b")
+        w2_g = keep.tile([P, H * PACK], BF16, name="w2_g", align_bytes=64, tag="stage")
+        for u in range(2):
+            nc.scalar.copy(dealt_view(w2_g)[:, u * (P // 2) : (u + 1) * (P // 2)], raw_view(w2_raw[u]))
+        w2_q = quantize(w2_g, H, "w2")
+        w1_g = keep.tile([P, H * PACK], BF16, name="w1_g", align_bytes=64, tag="w1_g")
+        nc.scalar.copy(dealt_view(w1_g)[:, : P // 2], raw_view(w1_raw[0]))
+        two_w = gather_words(two_l, "two_w", False, "two_w")
+
+        d_sb = []
+        for t in range(PACK):
+            d_ps = psum.tile([P, S], F32, name=f"d_ps{t}", tag=f"a{t}")
+            product(d_ps[:], w2_q, t, (two_w, two_b))
+            d_t = keep.tile([P, S], F32, name=f"d_sb{t}")
+            nc.scalar.copy(d_t[:], d_ps[:])
+            d_sb.append(d_t)
+
+        offs_w = gather_words(offs_l, "offs_w", False, "stage")
+        nc.vector.tensor_copy(dealt_view(w1_g)[:, P // 2 :], raw_view(w1_raw[1]))
+        cand_b = gather_bytes(cand_l, "cand_b", True, "w1_raw1")
+        w1_q = quantize(w1_g, H, "w1")
+        y_ps = []
+        for t in range(PACK):
+            y_t = psum.tile([P, S], F32, name=f"y_ps{t}", tag=f"b{t}")
+            product(y_t[:], w1_q, t, (offs_w, offs_b))
+            y_ps.append(y_t)
+        cand_w = gather_words(cand_l, "cand_w", True, "w1_g")
+
+        s_sb = [keep.tile([P, S], F32, name=f"s_sb{t}") for t in range(PACK)]
+        tops = keep.tile([P, 2 * PACK], F32, name="tops")
+        ea_bias = keep.tile([P, PACK], F32, name="ea_bias")
+        z_q = []
+
+        best = [keep.tile([P, PACK, HALF], F32, name=f"best{h}") for h in range(2)]
+        z_g = [keep.tile([P, HALF * PACK], BF16, name=f"z_g{h}", align_bytes=64) for h in range(2)]
+        pair = {}
+
+        def front(h, t):
+            cols = slice(HALF * h, HALF * (h + 1))
+            lcols = slice(HCOLS * h, HCOLS * (h + 1))
+            sg = keep.tile([P, HALF], F32, name=f"sg{h}{t}")
+            nc.scalar.activation(
+                sg[:], d_sb[t][:].indirect(n1_l[:, lcols]), ACT.Sigmoid,
+                bias=sg_bias[:, t : t + 1], scale=sl_c[:, t : t + 1],
+            )
+            dg = keep.tile([P, HALF], F32, name=f"dg{h}{t}")
+            nc.scalar.activation(dg[:], d_sb[t][:].indirect(n2_l[:, lcols]), ACT.Copy)
+            gated = keep.tile([P, HALF], F32, name=f"gated{h}{t}")
+            nc.vector.tensor_tensor(gated[:], y_ps[t][:, cols], sg[:], ALU.mult)
+            step = keep.tile([P, HALF], F32, name=f"step{h}{t}")
+            nc.vector.tensor_tensor(step[:], dg[:], d_sb[t][:, cols], ALU.subtract)
+            pair[h, t] = (gated, step)
+
+        def larger(h, t):
+            nc.vector.tensor_tensor(best[h][:, t, :], pair[h, t][0][:], pair[h, t][1][:], ALU.max)
+
+        def weave(h):
+            nc.vector.tensor_tensor(
+                z_g[h][:].rearrange("p (c i t) -> p c t i", i=4, t=PACK),
+                best[h][:].rearrange("p t (c i) -> p c t i", i=4),
+                gs_c[:].unsqueeze(1).unsqueeze(3).to_broadcast([P, HALF // 4, PACK, 4]),
+                ALU.mult,
+            )
+
+        def score(h, t):
+            s_ps = psum.tile([P, S], F32, name=f"s_ps{h}{t}", tag=f"{'ab'[h]}{t}")
+            product(s_ps[:, :HALF], (cand_w, cand_b), t, z_q[h])
+            nc.vector.tensor_scalar(
+                s_sb[t][:, HALF * h : HALF * (h + 1)], s_ps[:, :HALF], 0.0625, None, ALU.mult, ALU.max,
+                accum_out=tops[:, 2 * t + h : 2 * t + h + 1],
+            )
+
+        def exp_bias(t):
+            nc.vector.tensor_scalar(
+                ea_bias[:, t : t + 1], tops[:, 2 * t : 2 * t + 1],
+                tops[:, 2 * t + 1 : 2 * t + 2], neg_tau[:, t : t + 1], ALU.max, ALU.mult,
+            )
+
+        front(0, 0)
+        for t in range(1, PACK):
+            front(0, t)
+            larger(0, t - 1)
+        front(1, 0)
+        larger(0, 3)
+        front(1, 1)
+        weave(0)
+        larger(1, 0)
+        z_q.append(quantize(z_g[0], HALF, "z0"))
+        front(1, 2)
+        larger(1, 1)
+        front(1, 3)
+        larger(1, 2)
+        score(0, 0)
+        larger(1, 3)
+        score(0, 1)
+        weave(1)
+        score(0, 2)
+        z_q.append(quantize(z_g[1], HALF, "z1"))
+        score(0, 3)
+        score(1, 0)
+        for t in range(1, PACK):
+            score(1, t)
+            exp_bias(t - 1)
+        exp_bias(PACK - 1)
+
+        ea_all = keep.tile([P, PACK, S], F32, name="ea_all", tag="ea")
+        sq = [keep.tile([P, S], F32, name=f"sq{t}") for t in range(PACK)]
+        s3 = [keep.tile([P, S], F32, name=f"s3{t}") for t in range(PACK)]
+        diff = [keep.tile([P, S], F32, name=f"diff{t}") for t in range(PACK)]
+        for t in range(PACK):
+            for h in range(2):
+                cols = slice(HALF * h, HALF * (h + 1))
+                lcols = slice(HCOLS * h, HCOLS * (h + 1))
+                nc.scalar.activation(
+                    ea_all[:, t, cols], s_sb[t][:].indirect(n4_l[:, lcols]), ACT.Exp,
+                    bias=ea_bias[:, t : t + 1], scale=tau_c[:, t : t + 1],
+                )
+                nc.vector.tensor_copy(s3[t][:, cols], s_sb[t][:].indirect(n3_l[:, lcols]))
+                if h == 0 and t > 0:
+                    nc.vector.tensor_tensor(diff[t - 1][:], s_sb[t - 1][:], s3[t - 1][:], ALU.subtract)
+            if t > 0:
+                nc.scalar.activation(sq[t][:], ea_all[:, t, :], ACT.Square, bias=quarter[:])
+        nc.vector.scalar_tensor_tensor(sq[0][:], ea_all[:, 0, :], 0.5, ea_all[:, 0, :], ALU.add, ALU.mult)
+        nc.vector.tensor_tensor(diff[PACK - 1][:], s_sb[PACK - 1][:], s3[PACK - 1][:], ALU.subtract)
+
+        out_rows = out.rearrange("(p t) j -> p t j", t=PACK)
+        inv_all = keep.tile([P, PACK, S], F32, name="inv_all", tag="ea")
+        for t in range(PACK):
+            inv = inv_all[:, t, :]
+            if t == 0:
+                nc.scalar.activation(inv, sq[t][:], ACT.Abs_reciprocal_sqrt, scale=4.0, bias=quarter[:])
+            else:
+                nc.scalar.activation(inv, sq[t][:], ACT.Abs_reciprocal_sqrt, scale=4.0)
+            res = keep.tile([P, S], F32, name=f"res{t}")
+            nc.vector.tensor_tensor(res[:], diff[t][:], inv, ALU.mult)
+            nc.sync.dma_start(out_rows[:, t, :], res[:])

@@ -47,19 +47,19 @@ def tile_picked_twcmxbera_none_p_kernel(
         bytes_all = keep.tile([P, T], U8, name="bytes_all", align_bytes=64)
         nc.gpsimd.memset(bytes_all[:].bitcast(I32), 0)
         two_l = load_list(two, "two_l")
+        offs_l = load_list(offs, "offs_l")
+        words_all = keep.tile([P, T], I32, name="words_all", align_bytes=64)
+        nc.sync.dma_start(words_all[:], x_words[0].rearrange("p c r -> p (c r)").bitcast(I32))
         for q in range(4):
-            nc.scalar.dma_start(
+            nc.sync.dma_start(
                 bytes_all[32 * q : 32 * q + 4, :].bitcast(I32),
                 x_scales[0, 4 * q : 4 * q + 4, :].bitcast(I32),
             )
         w2_raw = [load_weight(w2[:, u * (H // 2) : (u + 1) * (H // 2)], f"w2_raw{u}") for u in range(2)]
-        offs_l = load_list(offs, "offs_l")
-        cand_l = load_list(cand, "cand_l")
-        words_all = keep.tile([P, T], I32, name="words_all", align_bytes=64)
-        nc.sync.dma_start(words_all[:], x_words[0].rearrange("p c r -> p (c r)").bitcast(I32))
         n1_l = load_list(n1, "n1_l")
         n2_l = load_list(n2, "n2_l")
         w1_raw = [load_weight(w1[:, u * (H // 2) : (u + 1) * (H // 2)], f"w1_raw{u}") for u in range(2)]
+        cand_l = load_list(cand, "cand_l")
         n4_l = load_list(n4, "n4_l")
         n3_l = load_list(n3, "n3_l")
         sl_c = load_column(sl, "sl_c")
@@ -112,36 +112,33 @@ def tile_picked_twcmxbera_none_p_kernel(
                 stop=True,
             )
 
+        two_w = gather_words(two_l, "two_w", False, "two_w")
+        offs_w = gather_words(offs_l, "offs_w", False, "offs_w")
         two_b = gather_bytes(two_l, "two_b", False, "two_b")
-        offs_b = gather_bytes(offs_l, "offs_b", False, "offs_b")
         w2_g = keep.tile([P, H * PACK], BF16, name="w2_g", align_bytes=64, tag="stage")
         for u in range(2):
             nc.scalar.copy(dealt_view(w2_g)[:, u * (P // 2) : (u + 1) * (P // 2)], raw_view(w2_raw[u]))
         w2_q = quantize(w2_g, H, "w2")
         w1_g = keep.tile([P, H * PACK], BF16, name="w1_g", align_bytes=64, tag="w1_g")
         nc.scalar.copy(dealt_view(w1_g)[:, : P // 2], raw_view(w1_raw[0]))
-        two_w = gather_words(two_l, "two_w", False, "two_w")
 
-        d_sb = []
+        d_ps = []
         for t in range(PACK):
-            d_ps = psum.tile([P, S], F32, name=f"d_ps{t}", tag=f"a{t}")
-            product(d_ps[:], w2_q, t, (two_w, two_b))
-            d_t = keep.tile([P, S], F32, name=f"d_sb{t}")
-            nc.scalar.copy(d_t[:], d_ps[:])
-            d_sb.append(d_t)
+            d_t = psum.tile([P, S], F32, name=f"d_ps{t}", tag=f"a{t}")
+            product(d_t[:], w2_q, t, (two_w, two_b))
+            d_ps.append(d_t)
+        d_sb = [keep.tile([P, S], F32, name=f"d_sb{t}") for t in range(PACK)]
 
-        offs_w = gather_words(offs_l, "offs_w", False, "stage")
+        offs_b = gather_bytes(offs_l, "offs_b", False, "stage")
         nc.vector.tensor_copy(dealt_view(w1_g)[:, P // 2 :], raw_view(w1_raw[1]))
-        cand_b = gather_bytes(cand_l, "cand_b", True, "w1_raw1")
         w1_q = quantize(w1_g, H, "w1")
         y_ps = []
         for t in range(PACK):
             y_t = psum.tile([P, S], F32, name=f"y_ps{t}", tag=f"b{t}")
             product(y_t[:], w1_q, t, (offs_w, offs_b))
             y_ps.append(y_t)
-        cand_w = gather_words(cand_l, "cand_w", True, "w1_g")
 
-        s_sb = [keep.tile([P, S], F32, name=f"s_sb{t}") for t in range(PACK)]
+        s_sb = [keep.tile([P, 2 * S], F32, name=f"s_sb{t}") for t in range(PACK)]
         tops = keep.tile([P, 2 * PACK], F32, name="tops")
         ea_bias = keep.tile([P, PACK], F32, name="ea_bias")
         z_q = []
@@ -153,21 +150,28 @@ def tile_picked_twcmxbera_none_p_kernel(
         def front(h, t):
             cols = slice(HALF * h, HALF * (h + 1))
             lcols = slice(HCOLS * h, HCOLS * (h + 1))
+            if h == 0:
+                nc.scalar.copy(d_sb[t][:], d_ps[t][:])
             sg = keep.tile([P, HALF], F32, name=f"sg{h}{t}")
             nc.scalar.activation(
                 sg[:], d_sb[t][:].indirect(n1_l[:, lcols]), ACT.Sigmoid,
                 bias=sg_bias[:, t : t + 1], scale=sl_c[:, t : t + 1],
             )
             dg = keep.tile([P, HALF], F32, name=f"dg{h}{t}")
-            nc.scalar.activation(dg[:], d_sb[t][:].indirect(n2_l[:, lcols]), ACT.Copy)
-            gated = keep.tile([P, HALF], F32, name=f"gated{h}{t}")
-            nc.vector.tensor_tensor(gated[:], y_ps[t][:, cols], sg[:], ALU.mult)
+            if (h, t) == (0, 1):
+                nc.vector.tensor_copy(dg[:], d_sb[t][:].indirect(n2_l[:, lcols]))
+            else:
+                nc.scalar.activation(dg[:], d_sb[t][:].indirect(n2_l[:, lcols]), ACT.Copy)
+            gated = s_sb[t][:, S + HALF * h : S + HALF * (h + 1)]
+            nc.vector.tensor_tensor(gated, y_ps[t][:, cols], sg[:], ALU.mult)
+            if (h, t) != (0, 0):
+                larger(*divmod(PACK * h + t - 1, PACK))
             step = keep.tile([P, HALF], F32, name=f"step{h}{t}")
             nc.vector.tensor_tensor(step[:], dg[:], d_sb[t][:, cols], ALU.subtract)
-            pair[h, t] = (gated, step)
+            pair[h, t] = (gated, step, dg)
 
         def larger(h, t):
-            nc.vector.tensor_tensor(best[h][:, t, :], pair[h, t][0][:], pair[h, t][1][:], ALU.max)
+            nc.vector.tensor_tensor(best[h][:, t, :], pair[h, t][0], pair[h, t][1][:], ALU.max)
 
         def weave(h):
             nc.vector.tensor_tensor(
@@ -192,19 +196,19 @@ def tile_picked_twcmxbera_none_p_kernel(
             )
 
         front(0, 0)
-        for t in range(1, PACK):
-            front(0, t)
-            larger(0, t - 1)
+        cand_b = gather_bytes(cand_l, "cand_b", True, "w1_raw1")
+        front(0, 1)
+        cand_w = gather_words(cand_l, "cand_w", True, "w1_g")
+        front(0, 2)
+        front(0, 3)
         front(1, 0)
-        larger(0, 3)
-        front(1, 1)
         weave(0)
-        larger(1, 0)
+        front(1, 1)
         z_q.append(quantize(z_g[0], HALF, "z0"))
         front(1, 2)
-        larger(1, 1)
         front(1, 3)
-        larger(1, 2)
+        warm_exp = keep.tile([P, 1], F32, name="warm_exp")
+        nc.scalar.activation(warm_exp[:], pair[1, 3][2][:, HALF - 1 :], ACT.Exp, scale=0.0)
         score(0, 0)
         larger(1, 3)
         score(0, 1)
@@ -223,29 +227,28 @@ def tile_picked_twcmxbera_none_p_kernel(
         s3 = [keep.tile([P, S], F32, name=f"s3{t}") for t in range(PACK)]
         diff = [keep.tile([P, S], F32, name=f"diff{t}") for t in range(PACK)]
         for t in range(PACK):
-            for h in range(2):
-                cols = slice(HALF * h, HALF * (h + 1))
-                lcols = slice(HCOLS * h, HCOLS * (h + 1))
-                nc.scalar.activation(
-                    ea_all[:, t, cols], s_sb[t][:].indirect(n4_l[:, lcols]), ACT.Exp,
-                    bias=ea_bias[:, t : t + 1], scale=tau_c[:, t : t + 1],
-                )
-                nc.vector.tensor_copy(s3[t][:, cols], s_sb[t][:].indirect(n3_l[:, lcols]))
-                if h == 0 and t > 0:
-                    nc.vector.tensor_tensor(diff[t - 1][:], s_sb[t - 1][:], s3[t - 1][:], ALU.subtract)
+            nc.scalar.activation(
+                ea_all[:, t, :], s_sb[t][:].indirect(n4_l[:]), ACT.Exp,
+                bias=ea_bias[:, t : t + 1], scale=tau_c[:, t : t + 1],
+            )
+            nc.vector.tensor_copy(s3[t][:], s_sb[t][:].indirect(n3_l[:]))
             if t > 0:
+                nc.vector.tensor_tensor(diff[t - 1][:], s_sb[t - 1][:, :S], s3[t - 1][:], ALU.subtract)
                 nc.scalar.activation(sq[t][:], ea_all[:, t, :], ACT.Square, bias=quarter[:])
-        nc.vector.scalar_tensor_tensor(sq[0][:], ea_all[:, 0, :], 0.5, ea_all[:, 0, :], ALU.add, ALU.mult)
-        nc.vector.tensor_tensor(diff[PACK - 1][:], s_sb[PACK - 1][:], s3[PACK - 1][:], ALU.subtract)
+            if t == 1:
+                nc.vector.scalar_tensor_tensor(sq[0][:], ea_all[:, 0, :], 0.5, ea_all[:, 0, :], ALU.add, ALU.mult)
+        nc.vector.tensor_tensor(diff[PACK - 1][:], s_sb[PACK - 1][:, :S], s3[PACK - 1][:], ALU.subtract)
 
         out_rows = out.rearrange("(p t) j -> p t j", t=PACK)
         inv_all = keep.tile([P, PACK, S], F32, name="inv_all", tag="ea")
-        for t in range(PACK):
-            inv = inv_all[:, t, :]
+        pieces = [(t, slice(0, S)) for t in range(PACK - 1)]
+        pieces.extend([(PACK - 1, slice(0, HALF)), (PACK - 1, slice(HALF, S))])
+        for n, (t, cols) in enumerate(pieces):
+            inv = inv_all[:, t, cols]
             if t == 0:
-                nc.scalar.activation(inv, sq[t][:], ACT.Abs_reciprocal_sqrt, scale=4.0, bias=quarter[:])
+                nc.scalar.activation(inv, sq[t][:, cols], ACT.Abs_reciprocal_sqrt, scale=4.0, bias=quarter[:])
             else:
-                nc.scalar.activation(inv, sq[t][:], ACT.Abs_reciprocal_sqrt, scale=4.0)
-            res = keep.tile([P, S], F32, name=f"res{t}")
-            nc.vector.tensor_tensor(res[:], diff[t][:], inv, ALU.mult)
-            nc.sync.dma_start(out_rows[:, t, :], res[:])
+                nc.scalar.activation(inv, sq[t][:, cols], ACT.Abs_reciprocal_sqrt, scale=4.0)
+            res = keep.tile([P, cols.stop - cols.start], F32, name=f"res{n}")
+            nc.vector.tensor_tensor(res[:], diff[t][:, cols], inv, ALU.mult)
+            nc.sync.dma_start(out_rows[:, t, cols], res[:])

@@ -139,6 +139,7 @@ def tile_picked_twcmxbera_none_p_kernel(
             y_ps.append(y_t)
 
         s_sb = [keep.tile([P, 2 * S], F32, name=f"s_sb{t}") for t in range(PACK)]
+        s_copy = [keep.tile([P, S], F32, name=f"s_copy{t}") for t in range(PACK)]
         tops = keep.tile([P, 2 * PACK], F32, name="tops")
         ea_bias = keep.tile([P, PACK], F32, name="ea_bias")
         z_q = []
@@ -188,9 +189,10 @@ def tile_picked_twcmxbera_none_p_kernel(
                 s_sb[t][:, HALF * h : HALF * (h + 1)], s_ps[:, :HALF], 0.0625, None, ALU.mult, ALU.max,
                 accum_out=tops[:, 2 * t + h : 2 * t + h + 1],
             )
+            nc.sync.dma_start(s_copy[t][:, HALF * h : HALF * (h + 1)], s_sb[t][:, HALF * h : HALF * (h + 1)])
 
         def exp_bias(t):
-            nc.vector.tensor_scalar(
+            nc.gpsimd.tensor_scalar(
                 ea_bias[:, t : t + 1], tops[:, 2 * t : 2 * t + 1],
                 tops[:, 2 * t + 1 : 2 * t + 2], neg_tau[:, t : t + 1], ALU.max, ALU.mult,
             )
@@ -216,28 +218,39 @@ def tile_picked_twcmxbera_none_p_kernel(
         score(0, 2)
         z_q.append(quantize(z_g[1], HALF, "z1"))
         score(0, 3)
-        score(1, 0)
-        for t in range(1, PACK):
+        for t in range(PACK):
             score(1, t)
-            exp_bias(t - 1)
-        exp_bias(PACK - 1)
+            exp_bias(t)
 
         ea_all = keep.tile([P, PACK, S], F32, name="ea_all", tag="ea")
         sq = [keep.tile([P, S], F32, name=f"sq{t}") for t in range(PACK)]
-        s3 = [keep.tile([P, S], F32, name=f"s3{t}") for t in range(PACK)]
         diff = [keep.tile([P, S], F32, name=f"diff{t}") for t in range(PACK)]
         for t in range(PACK):
             nc.scalar.activation(
                 ea_all[:, t, :], s_sb[t][:].indirect(n4_l[:]), ACT.Exp,
                 bias=ea_bias[:, t : t + 1], scale=tau_c[:, t : t + 1],
             )
-            nc.vector.tensor_copy(s3[t][:], s_sb[t][:].indirect(n3_l[:]))
-            if t > 0:
-                nc.vector.tensor_tensor(diff[t - 1][:], s_sb[t - 1][:, :S], s3[t - 1][:], ALU.subtract)
-                nc.scalar.activation(sq[t][:], ea_all[:, t, :], ACT.Square, bias=quarter[:])
-            if t == 1:
-                nc.vector.scalar_tensor_tensor(sq[0][:], ea_all[:, 0, :], 0.5, ea_all[:, 0, :], ALU.add, ALU.mult)
-        nc.vector.tensor_tensor(diff[PACK - 1][:], s_sb[PACK - 1][:, :S], s3[PACK - 1][:], ALU.subtract)
+        nc.scalar.activation(sq[PACK - 1][:], ea_all[:, PACK - 1, :], ACT.Square, bias=quarter[:])
+
+        def difference(h, t):
+            cols = slice(HALF * h, HALF * (h + 1))
+            lcols = slice(HCOLS * h, HCOLS * (h + 1))
+            nc.vector.tensor_tensor(
+                diff[t][:, cols], s_sb[t][:].indirect(n3_l[:, lcols]), s_copy[t][:, cols], ALU.subtract
+            )
+
+        def square(t):
+            nc.vector.scalar_tensor_tensor(sq[t][:], ea_all[:, t, :], 0.5, ea_all[:, t, :], ALU.add, ALU.mult)
+
+        difference(0, 0)
+        difference(0, 1)
+        square(0)
+        difference(0, 2)
+        difference(0, 3)
+        square(1)
+        square(2)
+        for t in range(PACK):
+            difference(1, t)
 
         out_rows = out.rearrange("(p t) j -> p t j", t=PACK)
         inv_all = keep.tile([P, PACK, S], F32, name="inv_all", tag="ea")
@@ -245,10 +258,10 @@ def tile_picked_twcmxbera_none_p_kernel(
         pieces.extend([(PACK - 1, slice(0, HALF)), (PACK - 1, slice(HALF, S))])
         for n, (t, cols) in enumerate(pieces):
             inv = inv_all[:, t, cols]
-            if t == 0:
+            if t < PACK - 1:
                 nc.scalar.activation(inv, sq[t][:, cols], ACT.Abs_reciprocal_sqrt, scale=4.0, bias=quarter[:])
             else:
                 nc.scalar.activation(inv, sq[t][:, cols], ACT.Abs_reciprocal_sqrt, scale=4.0)
             res = keep.tile([P, cols.stop - cols.start], F32, name=f"res{n}")
-            nc.vector.tensor_tensor(res[:], diff[t][:, cols], inv, ALU.mult)
+            nc.vector.scalar_tensor_tensor(res[:], diff[t][:, cols], -1.0, inv, ALU.mult, ALU.mult)
             nc.sync.dma_start(out_rows[:, t, cols], res[:])

from contextlib import ExitStack

import concourse.mybir as mybir

K, T, S, H, C = 512, 2048, 512, 512, 512
FLOPS = 3 * 2 * 512 * 512 * 512

F32 = mybir.dt.float32
BF16 = mybir.dt.bfloat16
I32 = mybir.dt.int32
U32 = mybir.dt.uint32
U16 = mybir.dt.uint16
U8 = mybir.dt.uint8
FP8X4 = mybir.dt.float8_e4m3fn_x4
ALU = mybir.AluOpType
ACT = mybir.ActivationFunctionType

P = 128
PACK = 4
HALF = S // 2
HCOLS = HALF // 16


def tile_picked_twcmxbera_none_p_kernel(
    tc, x_words, x_scales, w1, w2, sl, th, gs, tau, offs, two, n1, n2, cand, n3, n4, out
):
    nc = tc.nc
    with ExitStack() as ctx:
        keep = ctx.enter_context(tc.tile_pool(name="keep", bufs=1))
        psum = ctx.enter_context(tc.psum_pool(name="psum", bufs=1))

        def load_list(src, name):
            tile = keep.tile([P, S // 16], U16, name=name)
            nc.sync.dma_start(tile[:], src)
            return tile

        def load_column(src, name):
            tile = keep.tile([P, PACK], F32, name=name)
            nc.gpsimd.dma_start(tile[:], src.rearrange("(p t) o -> p (t o)", t=PACK))
            return tile

        def load_weight(src, name):
            tile = keep.tile([P, PACK, src.shape[1]], F32, name=name, tag=name, align_bytes=64)
            nc.sync.dma_start(tile[:], src.rearrange("(p j) h -> p j h", j=PACK))
            return tile

        bytes_all = keep.tile([P, T], U8, name="bytes_all", align_bytes=64)
        nc.gpsimd.memset(bytes_all[:].bitcast(I32), 0)
        two_l = load_list(two, "two_l")
        offs_l = load_list(offs, "offs_l")
        words_all = keep.tile([P, T], I32, name="words_all", align_bytes=64)
        nc.sync.dma_start(words_all[:], x_words[0].rearrange("p c r -> p (c r)").bitcast(I32))
        for q in range(4):
            nc.sync.dma_start(
                bytes_all[32 * q : 32 * q + 4, :].bitcast(I32),
                x_scales[0, 4 * q : 4 * q + 4, :].bitcast(I32),
            )
        w2_raw = [load_weight(w2[:, u * (H // 2) : (u + 1) * (H // 2)], f"w2_raw{u}") for u in range(2)]
        n1_l = load_list(n1, "n1_l")
        n2_l = load_list(n2, "n2_l")
        w1_raw = [load_weight(w1[:, u * (H // 2) : (u + 1) * (H // 2)], f"w1_raw{u}") for u in range(2)]
        cand_l = load_list(cand, "cand_l")
        n4_l = load_list(n4, "n4_l")
        n3_l = load_list(n3, "n3_l")
        sl_c = load_column(sl, "sl_c")
        th_c = load_column(th, "th_c")
        gs_c = load_column(gs, "gs_c")
        tau_c = load_column(tau, "tau_c")

        quarter = keep.tile([P, 1], F32, name="quarter")
        nc.gpsimd.memset(quarter[:], 0.25)
        slth = keep.tile([P, PACK], F32, name="slth")
        nc.gpsimd.tensor_tensor(slth[:], sl_c[:], th_c[:], ALU.mult)
        sg_bias = keep.tile([P, PACK], F32, name="sg_bias")
        nc.gpsimd.tensor_scalar(sg_bias[:], slth[:], -1.0, 0.0, ALU.mult, ALU.add)
        neg_tau = keep.tile([P, PACK], F32, name="neg_tau")
        nc.gpsimd.tensor_scalar(neg_tau[:], tau_c[:], -1.0, 0.0, ALU.mult, ALU.add)

        def gather_bytes(lst, name, dealt, tag):
            tile = keep.tile([P, S], U8, name=name, align_bytes=64, tag=tag)
            dst = tile[:].rearrange("p (t m) -> p m t", t=PACK) if dealt else tile[:]
            nc.vector.tensor_copy(dst, bytes_all[:].indirect(lst[:]))
            return tile

        def gather_words(lst, name, dealt, tag):
            tile = keep.tile([P, S], U32, name=name, align_bytes=64, tag=tag)
            dst = tile[:].rearrange("p (t m) -> p m t", t=PACK) if dealt else tile[:]
            nc.vector.tensor_copy(dst, words_all[:].bitcast(U32).indirect(lst[:]))
            return tile

        def dealt_view(grouped):
            return grouped[:].rearrange("p (t m j) -> p m j t", t=PACK, j=PACK)

        def raw_view(raw):
            return raw[:].rearrange("p j (m t) -> p m j t", t=PACK)

        def quantize(grouped, width, name):
            codes = keep.tile([P, width], U32, name=name + "_codes", align_bytes=64)
            scales = keep.tile([P, width], U8, name=name + "_scales", align_bytes=64)
            nc.vector.quantize_mx(out=codes[:].bitcast(FP8X4), scales=scales[:], in_=grouped[:])
            return codes, scales

        def product(acc, lhs, t, rhs):
            cols = slice(P * t, P * (t + 1))
            nc.tensor.matmul_mx(
                out=acc,
                lhsT=lhs[0][:, cols].bitcast(FP8X4),
                lhsT_scale=lhs[1][:, cols],
                rhs=rhs[0][:].bitcast(FP8X4),
                rhs_scale=rhs[1][:],
                start=True,
                stop=True,
            )

        two_w = gather_words(two_l, "two_w", False, "two_w")
        offs_w = gather_words(offs_l, "offs_w", False, "offs_w")
        two_b = gather_bytes(two_l, "two_b", False, "two_b")
        w2_g = keep.tile([P, H * PACK], BF16, name="w2_g", align_bytes=64, tag="stage")
        for u in range(2):
            nc.scalar.copy(dealt_view(w2_g)[:, u * (P // 2) : (u + 1) * (P // 2)], raw_view(w2_raw[u]))
        w2_q = quantize(w2_g, H, "w2")
        w1_g = keep.tile([P, H * PACK], BF16, name="w1_g", align_bytes=64, tag="w1_g")
        nc.scalar.copy(dealt_view(w1_g)[:, : P // 2], raw_view(w1_raw[0]))

        d_ps = []
        for t in range(PACK):
            d_t = psum.tile([P, S], F32, name=f"d_ps{t}", tag=f"a{t}")
            product(d_t[:], w2_q, t, (two_w, two_b))
            d_ps.append(d_t)
        d_sb = [keep.tile([P, S], F32, name=f"d_sb{t}") for t in range(PACK)]

        offs_b = gather_bytes(offs_l, "offs_b", False, "stage")
        nc.vector.tensor_copy(dealt_view(w1_g)[:, P // 2 :], raw_view(w1_raw[1]))
        w1_q = quantize(w1_g, H, "w1")
        y_ps = []
        for t in range(PACK):
            y_t = psum.tile([P, S], F32, name=f"y_ps{t}", tag=f"b{t}")
            product(y_t[:], w1_q, t, (offs_w, offs_b))
            y_ps.append(y_t)

        s_sb = [keep.tile([P, 2 * S], F32, name=f"s_sb{t}") for t in range(PACK)]
        s_copy = [keep.tile([P, S], F32, name=f"s_copy{t}") for t in range(PACK)]
        tops = keep.tile([P, 2 * PACK], F32, name="tops")
        ea_bias = keep.tile([P, PACK], F32, name="ea_bias")
        z_q = []

        best = [keep.tile([P, PACK, HALF], F32, name=f"best{h}") for h in range(2)]
        z_g = [keep.tile([P, HALF * PACK], BF16, name=f"z_g{h}", align_bytes=64) for h in range(2)]
        pair = {}

        def front(h, t):
            cols = slice(HALF * h, HALF * (h + 1))
            lcols = slice(HCOLS * h, HCOLS * (h + 1))
            if h == 0:
                nc.scalar.copy(d_sb[t][:], d_ps[t][:])
            sg = keep.tile([P, HALF], F32, name=f"sg{h}{t}")
            nc.scalar.activation(
                sg[:], d_sb[t][:].indirect(n1_l[:, lcols]), ACT.Sigmoid,
                bias=sg_bias[:, t : t + 1], scale=sl_c[:, t : t + 1],
            )
            dg = keep.tile([P, HALF], F32, name=f"dg{h}{t}")
            if (h, t) == (0, 1):
                nc.vector.tensor_copy(dg[:], d_sb[t][:].indirect(n2_l[:, lcols]))
            else:
                nc.scalar.activation(dg[:], d_sb[t][:].indirect(n2_l[:, lcols]), ACT.Copy)
            gated = s_sb[t][:, S + HALF * h : S + HALF * (h + 1)]
            nc.vector.tensor_tensor(gated, y_ps[t][:, cols], sg[:], ALU.mult)
            if (h, t) != (0, 0):
                larger(*divmod(PACK * h + t - 1, PACK))
            step = keep.tile([P, HALF], F32, name=f"step{h}{t}")
            nc.vector.tensor_tensor(step[:], dg[:], d_sb[t][:, cols], ALU.subtract)
            pair[h, t] = (gated, step, dg)

        def larger(h, t):
            nc.vector.tensor_tensor(best[h][:, t, :], pair[h, t][0], pair[h, t][1][:], ALU.max)

        def weave(h):
            nc.vector.tensor_tensor(
                z_g[h][:].rearrange("p (c i t) -> p c t i", i=4, t=PACK),
                best[h][:].rearrange("p t (c i) -> p c t i", i=4),
                gs_c[:].unsqueeze(1).unsqueeze(3).to_broadcast([P, HALF // 4, PACK, 4]),
                ALU.mult,
            )

        def score(h, t):
            s_ps = psum.tile([P, S], F32, name=f"s_ps{h}{t}", tag=f"{'ab'[h]}{t}")
            product(s_ps[:, :HALF], (cand_w, cand_b), t, z_q[h])
            nc.vector.tensor_scalar(
                s_sb[t][:, HALF * h : HALF * (h + 1)], s_ps[:, :HALF], 0.0625, None, ALU.mult, ALU.max,
                accum_out=tops[:, 2 * t + h : 2 * t + h + 1],
            )
            nc.sync.dma_start(s_copy[t][:, HALF * h : HALF * (h + 1)], s_sb[t][:, HALF * h : HALF * (h + 1)])

        def exp_bias(t):
            nc.gpsimd.tensor_scalar(
                ea_bias[:, t : t + 1], tops[:, 2 * t : 2 * t + 1],
                tops[:, 2 * t + 1 : 2 * t + 2], neg_tau[:, t : t + 1], ALU.max, ALU.mult,
            )

        front(0, 0)
        cand_b = gather_bytes(cand_l, "cand_b", True, "w1_raw1")
        front(0, 1)
        cand_w = gather_words(cand_l, "cand_w", True, "w1_g")
        front(0, 2)
        front(0, 3)
        front(1, 0)
        weave(0)
        front(1, 1)
        z_q.append(quantize(z_g[0], HALF, "z0"))
        front(1, 2)
        front(1, 3)
        warm_exp = keep.tile([P, 1], F32, name="warm_exp")
        nc.scalar.activation(warm_exp[:], pair[1, 3][2][:, HALF - 1 :], ACT.Exp, scale=0.0)
        score(0, 0)
        larger(1, 3)
        score(0, 1)
        weave(1)
        score(0, 2)
        z_q.append(quantize(z_g[1], HALF, "z1"))
        score(0, 3)
        for t in range(PACK):
            score(1, t)
            exp_bias(t)

        ea_all = keep.tile([P, PACK, S], F32, name="ea_all", tag="ea")
        sq = [keep.tile([P, S], F32, name=f"sq{t}") for t in range(PACK)]
        diff = [keep.tile([P, S], F32, name=f"diff{t}") for t in range(PACK)]
        for t in range(PACK):
            nc.scalar.activation(
                ea_all[:, t, :], s_sb[t][:].indirect(n4_l[:]), ACT.Exp,
                bias=ea_bias[:, t : t + 1], scale=tau_c[:, t : t + 1],
            )
        nc.scalar.activation(sq[PACK - 1][:], ea_all[:, PACK - 1, :], ACT.Square, bias=quarter[:])

        def difference(h, t):
            cols = slice(HALF * h, HALF * (h + 1))
            lcols = slice(HCOLS * h, HCOLS * (h + 1))
            nc.vector.tensor_tensor(
                diff[t][:, cols], s_sb[t][:].indirect(n3_l[:, lcols]), s_copy[t][:, cols], ALU.subtract
            )

        def square(t):
            nc.vector.scalar_tensor_tensor(sq[t][:], ea_all[:, t, :], 0.5, ea_all[:, t, :], ALU.add, ALU.mult)

        difference(0, 0)
        difference(0, 1)
        square(0)
        difference(0, 2)
        difference(0, 3)
        square(1)
        square(2)
        for t in range(PACK):
            difference(1, t)

        out_rows = out.rearrange("(p t) j -> p t j", t=PACK)
        inv_all = keep.tile([P, PACK, S], F32, name="inv_all", tag="ea")
        pieces = [(t, slice(0, S)) for t in range(PACK - 1)]
        pieces.extend([(PACK - 1, slice(0, HALF)), (PACK - 1, slice(HALF, S))])
        for n, (t, cols) in enumerate(pieces):
            inv = inv_all[:, t, cols]
            if t < PACK - 1:
                nc.scalar.activation(inv, sq[t][:, cols], ACT.Abs_reciprocal_sqrt, scale=4.0, bias=quarter[:])
            else:
                nc.scalar.activation(inv, sq[t][:, cols], ACT.Abs_reciprocal_sqrt, scale=4.0)
            res = keep.tile([P, cols.stop - cols.start], F32, name=f"res{n}")
            nc.vector.scalar_tensor_tensor(res[:], diff[t][:, cols], -1.0, inv, ALU.mult, ALU.mult)
            nc.sync.dma_start(out_rows[:, t, cols], res[:])
